import numpy as np
import ml_dtypes


def mxq(x, axis, fmt="e4m3"):
    dtype, down = {"e4m3": (ml_dtypes.float8_e4m3fn, 7), "e5m2": (ml_dtypes.float8_e5m2, 14)}[fmt]
    v = np.moveaxis(np.asarray(x, np.float32).astype(ml_dtypes.bfloat16).astype(np.float64), axis, -1)
    blocks = v.reshape(v.shape[:-1] + (-1, 32))
    amax = np.abs(blocks).max(-1, keepdims=True)
    byte = np.maximum(np.where(amax > 0, np.frexp(amax)[1] - 1 + 127, 0) - down, 1)
    scale = np.exp2(byte - 127.0)
    codes = (blocks / scale).astype(np.float32).astype(dtype).astype(np.float64)
    return np.moveaxis((codes * scale).reshape(v.shape), -1, axis)


WIDE = False


def mx_kscale(k):
    if not WIDE:
        return np.ones(k)
    levels = np.array([10, -10, 5, -5, 0])
    if k % 512:
        return np.exp2(np.random.permutation(np.resize(levels, k // 32))).repeat(32)
    a = np.empty((k // 512, 16))
    for p in range(k // 512):
        a[p, :8] = np.random.permutation(np.resize(levels, 8))
        for g in range(8):
            far = levels[np.abs(levels - a[p, g]) >= 10]
            a[p, g + 8] = far[np.random.randint(len(far))]
    return np.exp2(a.ravel()).repeat(32)


def f64(x):
    return np.asarray(x).astype(np.float64)


def striped8(idx):
    return np.concatenate([x.reshape(-1, 16).T for x in idx]).astype(np.uint16)


def runs(offs, k):
    lists = np.stack([offs[16 * r : 16 * r + 16].T.reshape(-1) for r in range(8)]).astype(np.int64)
    return lists[np.arange(k) % 512 // 64]


def pack_weight(w):
    k, n = w.shape
    w = f64(np.asarray(w, np.float32).astype(ml_dtypes.bfloat16)).reshape(k // 32, 32, n)
    amax = np.abs(w).max(1)
    byte = np.clip(np.where(amax > 0, np.frexp(amax)[1] - 1 + 127 - 7, 1), 1, 254)
    scaled = (w * np.exp2(127.0 - byte)[:, None, :]).reshape(k, n).astype(np.float32)
    words = np.ascontiguousarray(scaled.reshape(k // 512, 128, 4, n).transpose(0, 1, 3, 2)).astype(ml_dtypes.float8_e4m3fn).view(np.uint8)
    return words, np.ascontiguousarray(byte.astype(np.uint8).reshape(k // 512, 16, n))


def unpack_weight(words, scales):
    g, p, n, _ = words.shape
    vals = np.ascontiguousarray(words).view(ml_dtypes.float8_e4m3fn).astype(np.float64) * np.repeat(np.exp2(scales.astype(np.float64) - 127.0), 8, axis=1)[..., None]
    return vals.transpose(0, 1, 3, 2).reshape(g * 512, n)


K, T, S, H, N = 1024, 2048, 512, 512, 256


def setup_inputs():
    n = np.random.standard_normal
    s = mx_kscale(K)[:, None]
    u = mx_kscale(H)
    packed_xT = pack_weight(n((K, T)) * s)
    return {
        "x_words": packed_xT[0],
        "x_scales": packed_xT[1],
        "w1": (n((K, N)) / np.sqrt(2 * K) / s).astype(np.float32),
        "w2": (n((K, H)) / np.sqrt(K) / s * u).astype(np.float32),
        "w3": (n((H, N)) / np.sqrt(2 * H) / u[:, None]).astype(np.float32),
        "offs": striped8(np.stack([np.random.permutation(T)[:S] for _ in range(8)])),
    }


def reference(x_words, x_scales, w1, w2, w3, offs):
    xq = unpack_weight(x_words, x_scales)[np.arange(K)[:, None], runs(offs, K)]
    h = mxq(f64(w2), 0, "e4m3").T @ xq
    return mxq(f64(w1), 0, "e4m3").T @ xq + mxq(f64(w3), 0, "e4m3").T @ mxq(h, 0, "e4m3")

@@ -1,0 +1,177 @@
+from contextlib import ExitStack
+
+import concourse.mybir as mybir
+
+K, T, S, H, N = 1024, 2048, 512, 512, 256
+FLOPS = 2 * S * (K * H + K * N + H * N)
+
+F32 = mybir.dt.float32
+BF16 = mybir.dt.bfloat16
+I32 = mybir.dt.int32
+U32 = mybir.dt.uint32
+U16 = mybir.dt.uint16
+U8 = mybir.dt.uint8
+FP8X4 = mybir.dt.float8_e4m3fn_x4
+
+P = 128
+PACK = 4
+K_PASS = P * PACK
+PASSES = K // K_PASS
+PLANE_STEP = 8
+HALF = S // 2
+QUARTER = S // 4
+W2_VECTOR_SHARE = 80
+
+
+def tile_picked_phlora_none_p_kernel(tc, x_words, x_scales, w1, w2, w3, offs, out):
+    nc = tc.nc
+
+    with ExitStack() as ctx:
+        keep = ctx.enter_context(tc.tile_pool(name="keep", bufs=1))
+        psum = ctx.enter_context(tc.psum_pool(name="psum", bufs=1))
+
+        def sbuf(shape, dtype, name, tag=None):
+            return keep.tile(shape, dtype, name=name, tag=tag or name, align_bytes=64)
+
+        offsets = keep.tile([P, S // 16], U16, name="offsets")
+        nc.sync.dma_start(offsets[:], offs)
+
+        def load_rows(raw, w, z):
+            nc.sync.dma_start(raw, w[z * K_PASS : (z + 1) * K_PASS, :].rearrange("(p j) c -> p j c", j=PACK))
+
+        def load_words(z):
+            table = sbuf([P, T], U32, f"word_table{z}")
+            nc.sync.dma_start(table[:].bitcast(I32), x_words[z].rearrange("p c r -> p (c r)").bitcast(I32))
+            return table
+
+        scale_table = sbuf([P, T], U8, "scale_table", tag="scale_table_then_late_weights")
+        nc.vector.memset(scale_table[:].bitcast(I32), 0)
+        scale_rows = x_scales.bitcast(I32).rearrange("z (g i) c -> i g z c", i=2)
+        for i in range(2):
+            nc.scalar.dma_start(scale_table[i:P:PLANE_STEP, :].bitcast(I32), scale_rows[i])
+
+        w2_raw = [
+            sbuf([P, PACK, H], F32, "w2_raw0", tag="w2_raw0_then_picked_scales"),
+            sbuf([P, PACK, H], F32, "w2_raw1"),
+        ]
+        for z in range(PASSES):
+            load_rows(w2_raw[z][:], w2, z)
+        word_tables = [load_words(z) for z in range(PASSES)]
+
+        def quantize(grouped, name):
+            width = grouped.shape[1] // PACK
+            codes = sbuf([P, width], U32, name + "_codes")
+            scales = sbuf([P, width], U8, name + "_scales")
+            nc.vector.quantize_mx(out=codes[:].bitcast(FP8X4), scales=scales[:], in_=grouped[:])
+            return codes, scales
+
+        def prepare_w2(z):
+            grouped = sbuf([P, PACK * H], BF16, f"w2_grouped{z}")
+            dst = grouped[:].rearrange("p (t m j) -> p m j t", t=PACK, j=PACK)
+            src = w2_raw[z][:].rearrange("p j (m t) -> p m j t", t=PACK)
+            nc.scalar.copy(dst[:, W2_VECTOR_SHARE:], src[:, W2_VECTOR_SHARE:])
+            nc.vector.tensor_copy(dst[:, :W2_VECTOR_SHARE], src[:, :W2_VECTOR_SHARE])
+            return quantize(grouped, f"w2_{z}")
+
+        w2_mx = [prepare_w2(0)]
+
+        picked_scales = sbuf([P, S], U8, "picked_scales", tag="w2_raw0_then_picked_scales")
+        nc.vector.tensor_copy(picked_scales[:], scale_table[:].indirect(offsets[:]))
+        x_planes = sbuf([P, S], U8, "x_planes")
+        nc.vector.tensor_copy(x_planes[:].bitcast(I32), picked_scales[:].bitcast(I32))
+        for i in range(2):
+            nc.scalar.dma_start(
+                x_planes[2 + i : 2 + i + 105 : PLANE_STEP, :].bitcast(I32),
+                picked_scales[16 + i : 16 + i + 105 : PLANE_STEP, :].bitcast(I32),
+            )
+
+        late = sbuf([P, 3, PACK, N], F32, "late_weights", tag="scale_table_then_late_weights")
+        w1_raw0, w3_raw, w1_raw1 = late[:, 0], late[:, 1], late[:, 2]
+        load_rows(w1_raw0, w1, 0)
+        load_rows(w3_raw, w3, 0)
+        load_rows(w1_raw1, w1, 1)
+
+        w2_mx.append(prepare_w2(1))
+
+        def interleave(copy, raw, c0, c1, name):
+            grouped = sbuf([P, PACK * (c1 - c0)], BF16, name)
+            copy(
+                grouped[:].rearrange("p (c i j) -> p c j i", i=4, j=PACK),
+                raw[:, :, c0:c1].rearrange("p j (c i) -> p c j i", i=4),
+            )
+            return grouped
+
+        x0 = sbuf([P, S], U32, "x0")
+        nc.vector.tensor_copy(x0[:], word_tables[0][:].indirect(offsets[:]))
+        x1 = sbuf([P, S], U32, "x1")
+        for a in range(2):
+            nc.vector.tensor_copy(x1[:, a * HALF : (a + 1) * HALF], word_tables[1][:].indirect(offsets[:, a * 16 : (a + 1) * 16]))
+        x_codes = [x0, x1]
+
+        def product(acc, w_mx, c0, codes, plane, cols, start, stop):
+            nc.tensor.matmul_mx(
+                out=acc,
+                lhsT=w_mx[0][:, c0 : c0 + P].bitcast(FP8X4),
+                lhsT_scale=w_mx[1][:, c0 : c0 + P],
+                rhs=codes[:, cols].bitcast(FP8X4),
+                rhs_scale=plane[:, cols],
+                start=start,
+                stop=stop,
+            )
+
+        def x_plane(z):
+            return x_planes[PLANE_STEP * z :, :]
+
+        h_banks = [psum.tile([P, PACK, QUARTER], F32, name=f"h_bank{q}") for q in range(4)]
+        h_codes = sbuf([P, S], U32, "h_codes")
+        h_scales = sbuf([P, S], U8, "h_scales")
+
+        def h_pass(q, t, z):
+            cols = slice(q * QUARTER, (q + 1) * QUARTER)
+            product(h_banks[q][:, t, :], w2_mx[z], t * P, x_codes[z], x_plane(z), cols, z == 0, z == PASSES - 1)
+
+        for q in range(4):
+            h_pass(q, 0, 0)
+        h_grouped = []
+        for q in range(4):
+            h_pass(q, 0, 1)
+            for t in range(1, PACK):
+                for z in range(PASSES):
+                    h_pass(q, t, z)
+            grouped = sbuf([P, PACK * QUARTER], BF16, f"h_grouped{q}")
+            nc.scalar.copy(grouped[:].rearrange("p (n t) -> p n t", t=PACK), h_banks[q][:].rearrange("p t n -> p n t"))
+            h_grouped.append(grouped)
+
+        def quantize_h(q):
+            cols = slice(q * QUARTER, (q + 1) * QUARTER)
+            nc.vector.quantize_mx(out=h_codes[:, cols].bitcast(FP8X4), scales=h_scales[:, cols], in_=h_grouped[q][:])
+
+        w1_g0 = interleave(nc.vector.tensor_copy, w1_raw0, 0, N, "w1_g0")
+        quantize_h(0)
+        w1_mx0 = quantize(w1_g0, "w1_0")
+        w3_g = interleave(nc.vector.tensor_copy, w3_raw, 0, N, "w3_g")
+        quantize_h(1)
+        w3_mx = quantize(w3_g, "w3")
+        quantize_h(2)
+        w1_g1 = [
+            interleave(nc.vector.tensor_copy, w1_raw1, 0, P, "w1_g1a"),
+            interleave(nc.scalar.copy, w1_raw1, P, N, "w1_g1b"),
+        ]
+        quantize_h(3)
+        w1_mx1 = [quantize(w1_g1[m], f"w1_1_{m}") for m in range(2)]
+
+        out_banks = [[psum.tile([P, HALF], F32, name=f"out_bank{m}{a}") for a in range(2)] for m in range(2)]
+        halves = [slice(a * HALF, (a + 1) * HALF) for a in range(2)]
+        for m in range(2):
+            for a in range(2):
+                product(out_banks[m][a][:], w1_mx0, m * P, x0, x_plane(0), halves[a], True, False)
+        for a in range(2):
+            for m in range(2):
+                product(out_banks[m][a][:], w3_mx, m * P, h_codes, h_scales[:], halves[a], False, False)
+        for m in range(2):
+            for a in range(2):
+                product(out_banks[m][a][:], w1_mx1[m], 0, x1, x_plane(1), halves[a], False, True)
+            result = sbuf([P, S], F32, f"result{m}")
+            nc.scalar.copy(result[:, halves[0]], out_banks[m][0][:])
+            nc.vector.tensor_copy(result[:, halves[1]], out_banks[m][1][:])
+            nc.sync.dma_start(out[m * P : (m + 1) * P, :], result[:])

@@ -39,24 +39,24 @@ def tile_picked_phlora_none_p_kernel(tc, x_words, x_scales, w1, w2, w3, offs, ou
         def load_rows(raw, w, z):
             nc.sync.dma_start(raw, w[z * K_PASS : (z + 1) * K_PASS, :].rearrange("(p j) c -> p j c", j=PACK))
 
-        def load_words(z):
-            table = sbuf([P, T], U32, f"word_table{z}")
+        def load_words(z, tag=None):
+            table = sbuf([P, T], U32, f"word_table{z}", tag=tag)
             nc.sync.dma_start(table[:].bitcast(I32), x_words[z].rearrange("p c r -> p (c r)").bitcast(I32))
             return table
 
-        scale_table = sbuf([P, T], U8, "scale_table", tag="scale_table_then_late_weights")
+        scale_table = sbuf([P, T], U8, "scale_table", tag="scale_table_then_word_table1")
         nc.vector.memset(scale_table[:].bitcast(I32), 0)
         scale_rows = x_scales.bitcast(I32).rearrange("z (g i) c -> i g z c", i=2)
         for i in range(2):
-            nc.scalar.dma_start(scale_table[i:P:PLANE_STEP, :].bitcast(I32), scale_rows[i])
+            nc.sync.dma_start(scale_table[i:P:PLANE_STEP, :].bitcast(I32), scale_rows[i])
 
         w2_raw = [
-            sbuf([P, PACK, H], F32, "w2_raw0", tag="w2_raw0_then_picked_scales"),
-            sbuf([P, PACK, H], F32, "w2_raw1"),
+            sbuf([P, PACK, H], F32, "w2_raw0"),
+            sbuf([P, PACK, H], F32, "w2_raw1", tag="w2_raw1_then_late_weights"),
         ]
         for z in range(PASSES):
             load_rows(w2_raw[z][:], w2, z)
-        word_tables = [load_words(z) for z in range(PASSES)]
+        word_tables = [load_words(0)]
 
         def quantize(grouped, name):
             width = grouped.shape[1] // PACK
@@ -73,25 +73,23 @@ def tile_picked_phlora_none_p_kernel(tc, x_words, x_scales, w1, w2, w3, offs, ou
             nc.vector.tensor_copy(dst[:, :W2_VECTOR_SHARE], src[:, :W2_VECTOR_SHARE])
             return quantize(grouped, f"w2_{z}")
 
-        w2_mx = [prepare_w2(0)]
-
-        picked_scales = sbuf([P, S], U8, "picked_scales", tag="w2_raw0_then_picked_scales")
+        picked_scales = sbuf([P, S], U8, "picked_scales")
         nc.vector.tensor_copy(picked_scales[:], scale_table[:].indirect(offsets[:]))
         x_planes = sbuf([P, S], U8, "x_planes")
         nc.vector.tensor_copy(x_planes[:].bitcast(I32), picked_scales[:].bitcast(I32))
-        for i in range(2):
-            nc.scalar.dma_start(
-                x_planes[2 + i : 2 + i + 105 : PLANE_STEP, :].bitcast(I32),
-                picked_scales[16 + i : 16 + i + 105 : PLANE_STEP, :].bitcast(I32),
-            )
+        for z in range(PASSES):
+            for i in range(2):
+                row = PLANE_STEP * z + i
+                nc.sync.dma_start(x_planes[row + 2 : P : 32, :].bitcast(I32), picked_scales[row + 16 : P : 32, :].bitcast(I32))
+        word_tables.append(load_words(1, tag="scale_table_then_word_table1"))
 
-        late = sbuf([P, 3, PACK, N], F32, "late_weights", tag="scale_table_then_late_weights")
+        w2_mx = [prepare_w2(z) for z in range(PASSES)]
+
+        late = sbuf([P, 3, PACK, N], F32, "late_weights", tag="w2_raw1_then_late_weights")
         w1_raw0, w3_raw, w1_raw1 = late[:, 0], late[:, 1], late[:, 2]
         load_rows(w1_raw0, w1, 0)
         load_rows(w3_raw, w3, 0)
         load_rows(w1_raw1, w1, 1)
-
-        w2_mx.append(prepare_w2(1))
 
         def interleave(copy, raw, c0, c1, name):
             grouped = sbuf([P, PACK * (c1 - c0)], BF16, name)
@@ -130,38 +128,37 @@ def tile_picked_phlora_none_p_kernel(tc, x_words, x_scales, w1, w2, w3, offs, ou
             cols = slice(q * QUARTER, (q + 1) * QUARTER)
             product(h_banks[q][:, t, :], w2_mx[z], t * P, x_codes[z], x_plane(z), cols, z == 0, z == PASSES - 1)
 
+        out_banks = [[psum.tile([P, HALF], F32, name=f"out_bank{m}{a}") for a in range(2)] for m in range(2)]
+        halves = [slice(a * HALF, (a + 1) * HALF) for a in range(2)]
         for q in range(4):
             h_pass(q, 0, 0)
-        h_grouped = []
+        for m in range(2):
+            for a in range(2):
+                product(out_banks[m][a][:], w2_mx[0], 0, x0, x_plane(0), halves[a], True, True)
+        h_grouped = [sbuf([P, PACK * HALF], BF16, f"h_grouped{a}") for a in range(2)]
         for q in range(4):
             h_pass(q, 0, 1)
             for t in range(1, PACK):
                 for z in range(PASSES):
                     h_pass(q, t, z)
-            grouped = sbuf([P, PACK * QUARTER], BF16, f"h_grouped{q}")
-            nc.scalar.copy(grouped[:].rearrange("p (n t) -> p n t", t=PACK), h_banks[q][:].rearrange("p t n -> p n t"))
-            h_grouped.append(grouped)
+            part = h_grouped[q // 2][:, (q % 2) * PACK * QUARTER : (q % 2 + 1) * PACK * QUARTER]
+            nc.scalar.copy(part.rearrange("p (n t) -> p n t", t=PACK), h_banks[q][:].rearrange("p t n -> p n t"))
 
-        def quantize_h(q):
-            cols = slice(q * QUARTER, (q + 1) * QUARTER)
-            nc.vector.quantize_mx(out=h_codes[:, cols].bitcast(FP8X4), scales=h_scales[:, cols], in_=h_grouped[q][:])
+        def quantize_h(a):
+            nc.vector.quantize_mx(out=h_codes[:, halves[a]].bitcast(FP8X4), scales=h_scales[:, halves[a]], in_=h_grouped[a][:])
 
         w1_g0 = interleave(nc.vector.tensor_copy, w1_raw0, 0, N, "w1_g0")
-        quantize_h(0)
         w1_mx0 = quantize(w1_g0, "w1_0")
         w3_g = interleave(nc.vector.tensor_copy, w3_raw, 0, N, "w3_g")
-        quantize_h(1)
+        quantize_h(0)
         w3_mx = quantize(w3_g, "w3")
-        quantize_h(2)
         w1_g1 = [
             interleave(nc.vector.tensor_copy, w1_raw1, 0, P, "w1_g1a"),
             interleave(nc.scalar.copy, w1_raw1, P, N, "w1_g1b"),
         ]
-        quantize_h(3)
+        quantize_h(1)
         w1_mx1 = [quantize(w1_g1[m], f"w1_1_{m}") for m in range(2)]
 
-        out_banks = [[psum.tile([P, HALF], F32, name=f"out_bank{m}{a}") for a in range(2)] for m in range(2)]
-        halves = [slice(a * HALF, (a + 1) * HALF) for a in range(2)]
         for m in range(2):
             for a in range(2):
                 product(out_banks[m][a][:], w1_mx0, m * P, x0, x_plane(0), halves[a], True, False)

@@ -20,7 +20,7 @@ PASSES = K // K_PASS
 PLANE_STEP = 8
 HALF = S // 2
 QUARTER = S // 4
-W2_VECTOR_SHARE = 80
+W2_VECTOR_SHARE = (80, 80)
 
 
 def tile_picked_phlora_none_p_kernel(tc, x_words, x_scales, w1, w2, w3, offs, out):
@@ -51,27 +51,29 @@ def tile_picked_phlora_none_p_kernel(tc, x_words, x_scales, w1, w2, w3, offs, ou
             nc.sync.dma_start(scale_table[i:P:PLANE_STEP, :].bitcast(I32), scale_rows[i])
 
         w2_raw = [
-            sbuf([P, PACK, H], F32, "w2_raw0"),
-            sbuf([P, PACK, H], F32, "w2_raw1", tag="w2_raw1_then_late_weights"),
+            sbuf([P, PACK, H], F32, "w2_raw0", tag="w2_raw0_then_late_weights"),
+            sbuf([P, PACK, H], F32, "w2_raw1"),
         ]
         for z in range(PASSES):
             load_rows(w2_raw[z][:], w2, z)
         word_tables = [load_words(0)]
 
-        def quantize(grouped, name):
+        def quantize(grouped, name, codes_tag=None):
             width = grouped.shape[1] // PACK
-            codes = sbuf([P, width], U32, name + "_codes")
+            codes = sbuf([P, width], U32, name + "_codes", tag=codes_tag)
             scales = sbuf([P, width], U8, name + "_scales")
-            nc.vector.quantize_mx(out=codes[:].bitcast(FP8X4), scales=scales[:], in_=grouped[:])
+            nc.vector.quantize_mx(out=codes[:].bitcast(FP8X4), scales=scales[:], in_=grouped)
             return codes, scales
 
         def prepare_w2(z):
             grouped = sbuf([P, PACK * H], BF16, f"w2_grouped{z}")
             dst = grouped[:].rearrange("p (t m j) -> p m j t", t=PACK, j=PACK)
             src = w2_raw[z][:].rearrange("p j (m t) -> p m j t", t=PACK)
-            nc.scalar.copy(dst[:, W2_VECTOR_SHARE:], src[:, W2_VECTOR_SHARE:])
-            nc.vector.tensor_copy(dst[:, :W2_VECTOR_SHARE], src[:, :W2_VECTOR_SHARE])
-            return quantize(grouped, f"w2_{z}")
+            share = W2_VECTOR_SHARE[z]
+            if share < P:
+                nc.scalar.copy(dst[:, share:], src[:, share:])
+            nc.vector.tensor_copy(dst[:, :share], src[:, :share])
+            return quantize(grouped[:], f"w2_{z}")
 
         picked_scales = sbuf([P, S], U8, "picked_scales")
         nc.vector.tensor_copy(picked_scales[:], scale_table[:].indirect(offsets[:]))
@@ -83,21 +85,20 @@ def tile_picked_phlora_none_p_kernel(tc, x_words, x_scales, w1, w2, w3, offs, ou
                 nc.sync.dma_start(x_planes[row + 2 : P : 32, :].bitcast(I32), picked_scales[row + 16 : P : 32, :].bitcast(I32))
         word_tables.append(load_words(1, tag="scale_table_then_word_table1"))
 
-        w2_mx = [prepare_w2(z) for z in range(PASSES)]
+        w2_mx = [prepare_w2(0)]
 
-        late = sbuf([P, 3, PACK, N], F32, "late_weights", tag="w2_raw1_then_late_weights")
+        late = sbuf([P, 3, PACK, N], F32, "late_weights", tag="w2_raw0_then_late_weights")
         w1_raw0, w3_raw, w1_raw1 = late[:, 0], late[:, 1], late[:, 2]
         load_rows(w1_raw0, w1, 0)
         load_rows(w3_raw, w3, 0)
         load_rows(w1_raw1, w1, 1)
+        w2_mx.append(prepare_w2(1))
 
-        def interleave(copy, raw, c0, c1, name):
-            grouped = sbuf([P, PACK * (c1 - c0)], BF16, name)
+        def interleave(copy, grouped, raw):
             copy(
-                grouped[:].rearrange("p (c i j) -> p c j i", i=4, j=PACK),
-                raw[:, :, c0:c1].rearrange("p j (c i) -> p c j i", i=4),
+                grouped.rearrange("p (c i j) -> p c j i", i=4, j=PACK),
+                raw.rearrange("p j (c i) -> p c j i", i=4),
             )
-            return grouped
 
         x0 = sbuf([P, S], U32, "x0")
         nc.vector.tensor_copy(x0[:], word_tables[0][:].indirect(offsets[:]))
@@ -121,8 +122,6 @@ def tile_picked_phlora_none_p_kernel(tc, x_words, x_scales, w1, w2, w3, offs, ou
             return x_planes[PLANE_STEP * z :, :]
 
         h_banks = [psum.tile([P, PACK, QUARTER], F32, name=f"h_bank{q}") for q in range(4)]
-        h_codes = sbuf([P, S], U32, "h_codes")
-        h_scales = sbuf([P, S], U8, "h_scales")
 
         def h_pass(q, t, z):
             cols = slice(q * QUARTER, (q + 1) * QUARTER)
@@ -144,31 +143,45 @@ def tile_picked_phlora_none_p_kernel(tc, x_words, x_scales, w1, w2, w3, offs, ou
             part = h_grouped[q // 2][:, (q % 2) * PACK * QUARTER : (q % 2 + 1) * PACK * QUARTER]
             nc.scalar.copy(part.rearrange("p (n t) -> p n t", t=PACK), h_banks[q][:].rearrange("p t n -> p n t"))
 
-        def quantize_h(a):
-            nc.vector.quantize_mx(out=h_codes[:, halves[a]].bitcast(FP8X4), scales=h_scales[:, halves[a]], in_=h_grouped[a][:])
+        h_mx = []
 
-        w1_g0 = interleave(nc.vector.tensor_copy, w1_raw0, 0, N, "w1_g0")
-        w1_mx0 = quantize(w1_g0, "w1_0")
-        w3_g = interleave(nc.vector.tensor_copy, w3_raw, 0, N, "w3_g")
-        quantize_h(0)
-        w3_mx = quantize(w3_g, "w3")
-        w1_g1 = [
-            interleave(nc.vector.tensor_copy, w1_raw1, 0, P, "w1_g1a"),
-            interleave(nc.scalar.copy, w1_raw1, P, N, "w1_g1b"),
-        ]
-        quantize_h(1)
-        w1_mx1 = [quantize(w1_g1[m], f"w1_1_{m}") for m in range(2)]
+        w1_g0 = sbuf([P, PACK * N], BF16, "w1_g0")
+        interleave(nc.vector.tensor_copy, w1_g0[:], w1_raw0)
+        w1_mx0 = quantize(w1_g0[:], "w1_0")
+        first_g = sbuf([P, PACK * N], BF16, "first_g")
+        w3_gb = sbuf([P, PACK * P], BF16, "w3_gb", tag="w2_1_codes")
+        w1_gb = sbuf([P, PACK * P], BF16, "w1_gb")
+        interleave(nc.vector.tensor_copy, first_g[:, : PACK * P], w3_raw[:, :, :P])
+        h_mx.append(quantize(h_grouped[0][:], "h0"))
+        interleave(nc.vector.tensor_copy, first_g[:, PACK * P :], w1_raw1[:, :, :P])
+        first_mx = quantize(first_g[:], "first")
+        h_mx.append(quantize(h_grouped[1][:], "h1", codes_tag="first_g"))
+        interleave(nc.scalar.copy, w3_gb[:], w3_raw[:, :, P:])
+        interleave(nc.vector.tensor_copy, w1_gb[:], w1_raw1[:, :, P:])
+        w3_mxb = quantize(w3_gb[:], "w3_b")
+        w1_mxb = quantize(w1_gb[:], "w1_b")
 
+        def base_pass(m, a, w_mx, c0, stop):
+            product(out_banks[m][a][:], w_mx, c0, x1, x_plane(1), halves[a], False, stop)
+
+        def adapter_pass(m, a, w_mx, c0, stop):
+            product(out_banks[m][a][:], w_mx, c0, h_mx[a][0], h_mx[a][1][:], halves[0], False, stop)
+
+        results = [sbuf([P, S], F32, f"result{m}") for m in range(2)]
         for m in range(2):
             for a in range(2):
                 product(out_banks[m][a][:], w1_mx0, m * P, x0, x_plane(0), halves[a], True, False)
+        adapter_pass(0, 0, first_mx, 0, False)
+        base_pass(0, 0, first_mx, P, True)
+        base_pass(0, 1, first_mx, P, False)
+        adapter_pass(0, 1, first_mx, 0, True)
+        nc.scalar.copy(results[0][:, halves[0]], out_banks[0][0][:])
+        nc.vector.tensor_copy(results[0][:, halves[1]], out_banks[0][1][:])
+        nc.sync.dma_start(out[:P, :], results[0][:])
         for a in range(2):
-            for m in range(2):
-                product(out_banks[m][a][:], w3_mx, m * P, h_codes, h_scales[:], halves[a], False, False)
-        for m in range(2):
-            for a in range(2):
-                product(out_banks[m][a][:], w1_mx1[m], 0, x1, x_plane(1), halves[a], False, True)
-            result = sbuf([P, S], F32, f"result{m}")
-            nc.scalar.copy(result[:, halves[0]], out_banks[m][0][:])
-            nc.vector.tensor_copy(result[:, halves[1]], out_banks[m][1][:])
-            nc.sync.dma_start(out[m * P : (m + 1) * P, :], result[:])
+            adapter_pass(1, a, w3_mxb, 0, False)
+        for a in range(2):
+            base_pass(1, a, w1_mxb, 0, True)
+        nc.scalar.copy(results[1][:, halves[0]], out_banks[1][0][:])
+        nc.vector.tensor_copy(results[1][:, halves[1]], out_banks[1][1][:])
+        nc.sync.dma_start(out[P:, :], results[1][:])

@@ -131,9 +131,6 @@ def tile_picked_phlora_none_p_kernel(tc, x_words, x_scales, w1, w2, w3, offs, ou
         halves = [slice(a * HALF, (a + 1) * HALF) for a in range(2)]
         for q in range(4):
             h_pass(q, 0, 0)
-        for m in range(2):
-            for a in range(2):
-                product(out_banks[m][a][:], w2_mx[0], 0, x0, x_plane(0), halves[a], True, True)
         h_grouped = [sbuf([P, PACK * HALF], BF16, f"h_grouped{a}") for a in range(2)]
         for q in range(4):
             h_pass(q, 0, 1)

@@ -17,10 +17,14 @@ P = 128
 PACK = 4
 K_PASS = P * PACK
 PASSES = K // K_PASS
+LIST_ROWS = 16
+QUADRANT = 32
 PLANE_STEP = 8
 HALF = S // 2
 QUARTER = S // 4
-W2_VECTOR_SHARE = (80, 80)
+NEIGHBOURS = 4
+W2_VECTOR_SHARE = 80
+WARM_UP_PASSES = 3
 
 
 def tile_picked_phlora_none_p_kernel(tc, x_words, x_scales, w1, w2, w3, offs, out):
@@ -33,9 +37,6 @@ def tile_picked_phlora_none_p_kernel(tc, x_words, x_scales, w1, w2, w3, offs, ou
         def sbuf(shape, dtype, name, tag=None):
             return keep.tile(shape, dtype, name=name, tag=tag or name, align_bytes=64)
 
-        offsets = keep.tile([P, S // 16], U16, name="offsets")
-        nc.sync.dma_start(offsets[:], offs)
-
         def load_rows(raw, w, z):
             nc.sync.dma_start(raw, w[z * K_PASS : (z + 1) * K_PASS, :].rearrange("(p j) c -> p j c", j=PACK))
 
@@ -43,6 +44,9 @@ def tile_picked_phlora_none_p_kernel(tc, x_words, x_scales, w1, w2, w3, offs, ou
             table = sbuf([P, T], U32, f"word_table{z}", tag=tag)
             nc.sync.dma_start(table[:].bitcast(I32), x_words[z].rearrange("p c r -> p (c r)").bitcast(I32))
             return table
+
+        offsets = keep.tile([P, S // LIST_ROWS], U16, name="offsets")
+        nc.sync.dma_start(offsets[:], offs)
 
         scale_table = sbuf([P, T], U8, "scale_table", tag="scale_table_then_word_table1")
         nc.vector.memset(scale_table[:].bitcast(I32), 0)
@@ -69,10 +73,8 @@ def tile_picked_phlora_none_p_kernel(tc, x_words, x_scales, w1, w2, w3, offs, ou
             grouped = sbuf([P, PACK * H], BF16, f"w2_grouped{z}")
             dst = grouped[:].rearrange("p (t m j) -> p m j t", t=PACK, j=PACK)
             src = w2_raw[z][:].rearrange("p j (m t) -> p m j t", t=PACK)
-            share = W2_VECTOR_SHARE[z]
-            if share < P:
-                nc.scalar.copy(dst[:, share:], src[:, share:])
-            nc.vector.tensor_copy(dst[:, :share], src[:, :share])
+            nc.scalar.copy(dst[:, W2_VECTOR_SHARE:], src[:, W2_VECTOR_SHARE:])
+            nc.vector.tensor_copy(dst[:, :W2_VECTOR_SHARE], src[:, :W2_VECTOR_SHARE])
             return quantize(grouped[:], f"w2_{z}")
 
         picked_scales = sbuf([P, S], U8, "picked_scales")
@@ -82,13 +84,15 @@ def tile_picked_phlora_none_p_kernel(tc, x_words, x_scales, w1, w2, w3, offs, ou
         for z in range(PASSES):
             for i in range(2):
                 row = PLANE_STEP * z + i
-                nc.sync.dma_start(x_planes[row + 2 : P : 32, :].bitcast(I32), picked_scales[row + 16 : P : 32, :].bitcast(I32))
+                nc.sync.dma_start(
+                    x_planes[row + 2 : P : QUADRANT, :].bitcast(I32),
+                    picked_scales[row + LIST_ROWS : P : QUADRANT, :].bitcast(I32),
+                )
+
         word_tables.append(load_words(1, tag="scale_table_then_word_table1"))
-
         w2_mx = [prepare_w2(0)]
-
-        late = sbuf([P, 3, PACK, N], F32, "late_weights", tag="w2_raw0_then_late_weights")
-        w1_raw0, w3_raw, w1_raw1 = late[:, 0], late[:, 1], late[:, 2]
+        late_weights = sbuf([P, 3, PACK, N], F32, "late_weights", tag="w2_raw0_then_late_weights")
+        w1_raw0, w3_raw, w1_raw1 = late_weights[:, 0], late_weights[:, 1], late_weights[:, 2]
         load_rows(w1_raw0, w1, 0)
         load_rows(w3_raw, w3, 0)
         load_rows(w1_raw1, w1, 1)
@@ -96,41 +100,42 @@ def tile_picked_phlora_none_p_kernel(tc, x_words, x_scales, w1, w2, w3, offs, ou
 
         def interleave(copy, grouped, raw):
             copy(
-                grouped.rearrange("p (c i j) -> p c j i", i=4, j=PACK),
-                raw.rearrange("p j (c i) -> p c j i", i=4),
+                grouped.rearrange("p (c n j) -> p c j n", n=NEIGHBOURS, j=PACK),
+                raw.rearrange("p j (c n) -> p c j n", n=NEIGHBOURS),
             )
 
-        x0 = sbuf([P, S], U32, "x0")
-        nc.vector.tensor_copy(x0[:], word_tables[0][:].indirect(offsets[:]))
-        x1 = sbuf([P, S], U32, "x1")
-        for a in range(2):
-            nc.vector.tensor_copy(x1[:, a * HALF : (a + 1) * HALF], word_tables[1][:].indirect(offsets[:, a * 16 : (a + 1) * 16]))
-        x_codes = [x0, x1]
+        halves = [slice(a * HALF, (a + 1) * HALF) for a in range(2)]
+        list_halves = [slice(a * HALF // LIST_ROWS, (a + 1) * HALF // LIST_ROWS) for a in range(2)]
+        x_codes = [sbuf([P, S], U32, f"x_codes{z}") for z in range(PASSES)]
+        for z in range(PASSES):
+            for a in range(2):
+                nc.vector.tensor_copy(x_codes[z][:, halves[a]], word_tables[z][:].indirect(offsets[:, list_halves[a]]))
+        x_mx = [(x_codes[z], x_planes[PLANE_STEP * z :, :]) for z in range(PASSES)]
 
-        def product(acc, w_mx, c0, codes, plane, cols, start, stop):
+        def product(acc, w_mx, w_col, moving_mx, cols, start, stop):
             nc.tensor.matmul_mx(
                 out=acc,
-                lhsT=w_mx[0][:, c0 : c0 + P].bitcast(FP8X4),
-                lhsT_scale=w_mx[1][:, c0 : c0 + P],
-                rhs=codes[:, cols].bitcast(FP8X4),
-                rhs_scale=plane[:, cols],
+                lhsT=w_mx[0][:, w_col : w_col + P].bitcast(FP8X4),
+                lhsT_scale=w_mx[1][:, w_col : w_col + P],
+                rhs=moving_mx[0][:, cols].bitcast(FP8X4),
+                rhs_scale=moving_mx[1][:, cols],
                 start=start,
                 stop=stop,
             )
 
-        def x_plane(z):
-            return x_planes[PLANE_STEP * z :, :]
-
         h_banks = [psum.tile([P, PACK, QUARTER], F32, name=f"h_bank{q}") for q in range(4)]
+        out_banks = [[psum.tile([P, HALF], F32, name=f"out_bank{m}{a}") for a in range(2)] for m in range(2)]
 
         def h_pass(q, t, z):
             cols = slice(q * QUARTER, (q + 1) * QUARTER)
-            product(h_banks[q][:, t, :], w2_mx[z], t * P, x_codes[z], x_plane(z), cols, z == 0, z == PASSES - 1)
+            product(h_banks[q][:, t, :], w2_mx[z], t * P, x_mx[z], cols, z == 0, z == PASSES - 1)
 
-        out_banks = [[psum.tile([P, HALF], F32, name=f"out_bank{m}{a}") for a in range(2)] for m in range(2)]
-        halves = [slice(a * HALF, (a + 1) * HALF) for a in range(2)]
-        for q in range(4):
-            h_pass(q, 0, 0)
+        for a in range(2):
+            for q in (2 * a, 2 * a + 1):
+                h_pass(q, 0, 0)
+            for turn in range(WARM_UP_PASSES):
+                product(out_banks[turn % 2][a][:], w2_mx[0], 0, x_mx[0], halves[a], True, True)
+
         h_grouped = [sbuf([P, PACK * HALF], BF16, f"h_grouped{a}") for a in range(2)]
         for q in range(4):
             h_pass(q, 0, 1)
@@ -140,45 +145,45 @@ def tile_picked_phlora_none_p_kernel(tc, x_words, x_scales, w1, w2, w3, offs, ou
             part = h_grouped[q // 2][:, (q % 2) * PACK * QUARTER : (q % 2 + 1) * PACK * QUARTER]
             nc.scalar.copy(part.rearrange("p (n t) -> p n t", t=PACK), h_banks[q][:].rearrange("p t n -> p n t"))
 
-        h_mx = []
+        w1_grouped0 = sbuf([P, PACK * N], BF16, "w1_grouped0")
+        interleave(nc.vector.tensor_copy, w1_grouped0[:], w1_raw0)
+        w1_mx0 = quantize(w1_grouped0[:], "w1_0")
+        upper_grouped = sbuf([P, PACK * 2 * P], BF16, "upper_grouped")
+        w3_lower_grouped = sbuf([P, PACK * P], BF16, "w3_lower_grouped", tag="w2_1_codes")
+        w1_lower_grouped = sbuf([P, PACK * P], BF16, "w1_lower_grouped")
+        interleave(nc.vector.tensor_copy, upper_grouped[:, : PACK * P], w3_raw[:, :, :P])
+        h_mx = [quantize(h_grouped[0][:], "h0")]
+        interleave(nc.vector.tensor_copy, upper_grouped[:, PACK * P :], w1_raw1[:, :, :P])
+        upper_mx = quantize(upper_grouped[:], "upper")
+        h_mx.append(quantize(h_grouped[1][:], "h1", codes_tag="upper_grouped"))
+        interleave(nc.scalar.copy, w3_lower_grouped[:], w3_raw[:, :, P:])
+        interleave(nc.vector.tensor_copy, w1_lower_grouped[:], w1_raw1[:, :, P:])
+        w3_lower_mx = quantize(w3_lower_grouped[:], "w3_lower")
+        w1_lower_mx = quantize(w1_lower_grouped[:], "w1_lower")
 
-        w1_g0 = sbuf([P, PACK * N], BF16, "w1_g0")
-        interleave(nc.vector.tensor_copy, w1_g0[:], w1_raw0)
-        w1_mx0 = quantize(w1_g0[:], "w1_0")
-        first_g = sbuf([P, PACK * N], BF16, "first_g")
-        w3_gb = sbuf([P, PACK * P], BF16, "w3_gb", tag="w2_1_codes")
-        w1_gb = sbuf([P, PACK * P], BF16, "w1_gb")
-        interleave(nc.vector.tensor_copy, first_g[:, : PACK * P], w3_raw[:, :, :P])
-        h_mx.append(quantize(h_grouped[0][:], "h0"))
-        interleave(nc.vector.tensor_copy, first_g[:, PACK * P :], w1_raw1[:, :, :P])
-        first_mx = quantize(first_g[:], "first")
-        h_mx.append(quantize(h_grouped[1][:], "h1", codes_tag="first_g"))
-        interleave(nc.scalar.copy, w3_gb[:], w3_raw[:, :, P:])
-        interleave(nc.vector.tensor_copy, w1_gb[:], w1_raw1[:, :, P:])
-        w3_mxb = quantize(w3_gb[:], "w3_b")
-        w1_mxb = quantize(w1_gb[:], "w1_b")
+        def base_pass(m, a, w_mx, w_col, stop):
+            product(out_banks[m][a][:], w_mx, w_col, x_mx[1], halves[a], False, stop)
 
-        def base_pass(m, a, w_mx, c0, stop):
-            product(out_banks[m][a][:], w_mx, c0, x1, x_plane(1), halves[a], False, stop)
-
-        def adapter_pass(m, a, w_mx, c0, stop):
-            product(out_banks[m][a][:], w_mx, c0, h_mx[a][0], h_mx[a][1][:], halves[0], False, stop)
+        def adapter_pass(m, a, w_mx, stop):
+            product(out_banks[m][a][:], w_mx, 0, h_mx[a], slice(0, HALF), False, stop)
 
         results = [sbuf([P, S], F32, f"result{m}") for m in range(2)]
         for m in range(2):
             for a in range(2):
-                product(out_banks[m][a][:], w1_mx0, m * P, x0, x_plane(0), halves[a], True, False)
-        adapter_pass(0, 0, first_mx, 0, False)
-        base_pass(0, 0, first_mx, P, True)
-        base_pass(0, 1, first_mx, P, False)
-        adapter_pass(0, 1, first_mx, 0, True)
-        nc.scalar.copy(results[0][:, halves[0]], out_banks[0][0][:])
-        nc.vector.tensor_copy(results[0][:, halves[1]], out_banks[0][1][:])
+                product(out_banks[m][a][:], w1_mx0, m * P, x_mx[0], halves[a], True, False)
+
+        adapter_pass(0, 0, upper_mx, False)
+        base_pass(0, 0, upper_mx, P, True)
+        base_pass(0, 1, upper_mx, P, False)
+        adapter_pass(0, 1, upper_mx, True)
+        for a in range(2):
+            nc.scalar.copy(results[0][:, halves[a]], out_banks[0][a][:])
         nc.sync.dma_start(out[:P, :], results[0][:])
+
         for a in range(2):
-            adapter_pass(1, a, w3_mxb, 0, False)
+            adapter_pass(1, a, w3_lower_mx, False)
         for a in range(2):
-            base_pass(1, a, w1_mxb, 0, True)
+            base_pass(1, a, w1_lower_mx, 0, True)
         nc.scalar.copy(results[1][:, halves[0]], out_banks[1][0][:])
         nc.vector.tensor_copy(results[1][:, halves[1]], out_banks[1][1][:])
         nc.sync.dma_start(out[P:, :], results[1][:])

from contextlib import ExitStack

import concourse.mybir as mybir

K, T, S, H, N = 1024, 2048, 512, 512, 256
FLOPS = 2 * S * (K * H + K * N + H * N)

F32 = mybir.dt.float32
BF16 = mybir.dt.bfloat16
I32 = mybir.dt.int32
U32 = mybir.dt.uint32
U16 = mybir.dt.uint16
U8 = mybir.dt.uint8
FP8X4 = mybir.dt.float8_e4m3fn_x4

P = 128
PACK = 4
K_PASS = P * PACK
PASSES = K // K_PASS
LIST_ROWS = 16
QUADRANT = 32
PLANE_STEP = 8
HALF = S // 2
QUARTER = S // 4
NEIGHBOURS = 4
W2_VECTOR_SHARE = 80
WARM_UP_PASSES = 3


def tile_picked_phlora_none_p_kernel(tc, x_words, x_scales, w1, w2, w3, offs, out):
    nc = tc.nc

    with ExitStack() as ctx:
        keep = ctx.enter_context(tc.tile_pool(name="keep", bufs=1))
        psum = ctx.enter_context(tc.psum_pool(name="psum", bufs=1))

        def sbuf(shape, dtype, name, tag=None):
            return keep.tile(shape, dtype, name=name, tag=tag or name, align_bytes=64)

        def load_rows(raw, w, z):
            nc.sync.dma_start(raw, w[z * K_PASS : (z + 1) * K_PASS, :].rearrange("(p j) c -> p j c", j=PACK))

        def load_words(z, tag=None):
            table = sbuf([P, T], U32, f"word_table{z}", tag=tag)
            nc.sync.dma_start(table[:].bitcast(I32), x_words[z].rearrange("p c r -> p (c r)").bitcast(I32))
            return table

        offsets = keep.tile([P, S // LIST_ROWS], U16, name="offsets")
        nc.sync.dma_start(offsets[:], offs)

        scale_table = sbuf([P, T], U8, "scale_table", tag="scale_table_then_word_table1")
        nc.vector.memset(scale_table[:].bitcast(I32), 0)
        scale_rows = x_scales.bitcast(I32).rearrange("z (g i) c -> i g z c", i=2)
        for i in range(2):
            nc.sync.dma_start(scale_table[i:P:PLANE_STEP, :].bitcast(I32), scale_rows[i])

        w2_raw = [
            sbuf([P, PACK, H], F32, "w2_raw0", tag="w2_raw0_then_late_weights"),
            sbuf([P, PACK, H], F32, "w2_raw1"),
        ]
        for z in range(PASSES):
            load_rows(w2_raw[z][:], w2, z)
        word_tables = [load_words(0)]

        def quantize(grouped, name, codes_tag=None):
            width = grouped.shape[1] // PACK
            codes = sbuf([P, width], U32, name + "_codes", tag=codes_tag)
            scales = sbuf([P, width], U8, name + "_scales")
            nc.vector.quantize_mx(out=codes[:].bitcast(FP8X4), scales=scales[:], in_=grouped)
            return codes, scales

        def prepare_w2(z):
            grouped = sbuf([P, PACK * H], BF16, f"w2_grouped{z}")
            dst = grouped[:].rearrange("p (t m j) -> p m j t", t=PACK, j=PACK)
            src = w2_raw[z][:].rearrange("p j (m t) -> p m j t", t=PACK)
            nc.scalar.copy(dst[:, W2_VECTOR_SHARE:], src[:, W2_VECTOR_SHARE:])
            nc.vector.tensor_copy(dst[:, :W2_VECTOR_SHARE], src[:, :W2_VECTOR_SHARE])
            return quantize(grouped[:], f"w2_{z}")

        picked_scales = sbuf([P, S], U8, "picked_scales")
        nc.vector.tensor_copy(picked_scales[:], scale_table[:].indirect(offsets[:]))
        x_planes = sbuf([P, S], U8, "x_planes")
        nc.vector.tensor_copy(x_planes[:].bitcast(I32), picked_scales[:].bitcast(I32))
        for z in range(PASSES):
            for i in range(2):
                row = PLANE_STEP * z + i
                nc.sync.dma_start(
                    x_planes[row + 2 : P : QUADRANT, :].bitcast(I32),
                    picked_scales[row + LIST_ROWS : P : QUADRANT, :].bitcast(I32),
                )

        word_tables.append(load_words(1, tag="scale_table_then_word_table1"))
        w2_mx = [prepare_w2(0)]
        late_weights = sbuf([P, 3, PACK, N], F32, "late_weights", tag="w2_raw0_then_late_weights")
        w1_raw0, w3_raw, w1_raw1 = late_weights[:, 0], late_weights[:, 1], late_weights[:, 2]
        load_rows(w1_raw0, w1, 0)
        load_rows(w3_raw, w3, 0)
        load_rows(w1_raw1, w1, 1)
        w2_mx.append(prepare_w2(1))

        def interleave(copy, grouped, raw):
            copy(
                grouped.rearrange("p (c n j) -> p c j n", n=NEIGHBOURS, j=PACK),
                raw.rearrange("p j (c n) -> p c j n", n=NEIGHBOURS),
            )

        halves = [slice(a * HALF, (a + 1) * HALF) for a in range(2)]
        list_halves = [slice(a * HALF // LIST_ROWS, (a + 1) * HALF // LIST_ROWS) for a in range(2)]
        x_codes = [sbuf([P, S], U32, f"x_codes{z}") for z in range(PASSES)]
        for z in range(PASSES):
            for a in range(2):
                nc.vector.tensor_copy(x_codes[z][:, halves[a]], word_tables[z][:].indirect(offsets[:, list_halves[a]]))
        x_mx = [(x_codes[z], x_planes[PLANE_STEP * z :, :]) for z in range(PASSES)]

        def product(acc, w_mx, w_col, moving_mx, cols, start, stop):
            nc.tensor.matmul_mx(
                out=acc,
                lhsT=w_mx[0][:, w_col : w_col + P].bitcast(FP8X4),
                lhsT_scale=w_mx[1][:, w_col : w_col + P],
                rhs=moving_mx[0][:, cols].bitcast(FP8X4),
                rhs_scale=moving_mx[1][:, cols],
                start=start,
                stop=stop,
            )

        h_banks = [psum.tile([P, PACK, QUARTER], F32, name=f"h_bank{q}") for q in range(4)]
        out_banks = [[psum.tile([P, HALF], F32, name=f"out_bank{m}{a}") for a in range(2)] for m in range(2)]

        def h_pass(q, t, z):
            cols = slice(q * QUARTER, (q + 1) * QUARTER)
            product(h_banks[q][:, t, :], w2_mx[z], t * P, x_mx[z], cols, z == 0, z == PASSES - 1)

        for a in range(2):
            for q in (2 * a, 2 * a + 1):
                h_pass(q, 0, 0)
            for turn in range(WARM_UP_PASSES):
                product(out_banks[turn % 2][a][:], w2_mx[0], 0, x_mx[0], halves[a], True, True)

        h_grouped = [sbuf([P, PACK * HALF], BF16, f"h_grouped{a}") for a in range(2)]
        for q in range(4):
            h_pass(q, 0, 1)
            for t in range(1, PACK):
                for z in range(PASSES):
                    h_pass(q, t, z)
            part = h_grouped[q // 2][:, (q % 2) * PACK * QUARTER : (q % 2 + 1) * PACK * QUARTER]
            nc.scalar.copy(part.rearrange("p (n t) -> p n t", t=PACK), h_banks[q][:].rearrange("p t n -> p n t"))

        w1_grouped0 = sbuf([P, PACK * N], BF16, "w1_grouped0")
        interleave(nc.vector.tensor_copy, w1_grouped0[:], w1_raw0)
        w1_mx0 = quantize(w1_grouped0[:], "w1_0")
        upper_grouped = sbuf([P, PACK * 2 * P], BF16, "upper_grouped")
        w3_lower_grouped = sbuf([P, PACK * P], BF16, "w3_lower_grouped", tag="w2_1_codes")
        w1_lower_grouped = sbuf([P, PACK * P], BF16, "w1_lower_grouped")
        interleave(nc.vector.tensor_copy, upper_grouped[:, : PACK * P], w3_raw[:, :, :P])
        h_mx = [quantize(h_grouped[0][:], "h0")]
        interleave(nc.vector.tensor_copy, upper_grouped[:, PACK * P :], w1_raw1[:, :, :P])
        upper_mx = quantize(upper_grouped[:], "upper")
        h_mx.append(quantize(h_grouped[1][:], "h1", codes_tag="upper_grouped"))
        interleave(nc.scalar.copy, w3_lower_grouped[:], w3_raw[:, :, P:])
        interleave(nc.vector.tensor_copy, w1_lower_grouped[:], w1_raw1[:, :, P:])
        w3_lower_mx = quantize(w3_lower_grouped[:], "w3_lower")
        w1_lower_mx = quantize(w1_lower_grouped[:], "w1_lower")

        def base_pass(m, a, w_mx, w_col, stop):
            product(out_banks[m][a][:], w_mx, w_col, x_mx[1], halves[a], False, stop)

        def adapter_pass(m, a, w_mx, stop):
            product(out_banks[m][a][:], w_mx, 0, h_mx[a], slice(0, HALF), False, stop)

        results = [sbuf([P, S], F32, f"result{m}") for m in range(2)]
        for m in range(2):
            for a in range(2):
                product(out_banks[m][a][:], w1_mx0, m * P, x_mx[0], halves[a], True, False)

        adapter_pass(0, 0, upper_mx, False)
        base_pass(0, 0, upper_mx, P, True)
        base_pass(0, 1, upper_mx, P, False)
        adapter_pass(0, 1, upper_mx, True)
        for a in range(2):
            nc.scalar.copy(results[0][:, halves[a]], out_banks[0][a][:])
        nc.sync.dma_start(out[:P, :], results[0][:])

        for a in range(2):
            adapter_pass(1, a, w3_lower_mx, False)
        for a in range(2):
            base_pass(1, a, w1_lower_mx, 0, True)
        nc.scalar.copy(results[1][:, halves[0]], out_banks[1][0][:])
        nc.vector.tensor_copy(results[1][:, halves[1]], out_banks[1][1][:])
        nc.sync.dma_start(out[P:, :], results[1][:])
